import numpy as np
import ml_dtypes


def mxq(x, axis, fmt="e4m3"):
    dtype, down = {"e4m3": (ml_dtypes.float8_e4m3fn, 7), "e5m2": (ml_dtypes.float8_e5m2, 14)}[fmt]
    v = np.moveaxis(np.asarray(x, np.float32).astype(ml_dtypes.bfloat16).astype(np.float64), axis, -1)
    blocks = v.reshape(v.shape[:-1] + (-1, 32))
    amax = np.abs(blocks).max(-1, keepdims=True)
    byte = np.maximum(np.where(amax > 0, np.frexp(amax)[1] - 1 + 127, 0) - down, 1)
    scale = np.exp2(byte - 127.0)
    codes = (blocks / scale).astype(np.float32).astype(dtype).astype(np.float64)
    return np.moveaxis((codes * scale).reshape(v.shape), -1, axis)


WIDE = False


def mx_kscale(k):
    if not WIDE:
        return np.ones(k)
    levels = np.array([30, -30])
    if k % 512:
        return np.exp2(np.random.permutation(np.resize(levels, k // 32))).repeat(32)
    a = np.empty((k // 512, 16))
    for p in range(k // 512):
        a[p, :8] = np.random.permutation(np.resize(levels, 8))
        for g in range(8):
            far = levels[np.abs(levels - a[p, g]) >= 10]
            a[p, g + 8] = far[np.random.randint(len(far))]
    return np.exp2(a.ravel()).repeat(32)


def f64(x):
    return np.asarray(x).astype(np.float64)


def striped(idx):
    return np.tile(np.asarray(idx).reshape(-1, 16).T, (8, 1)).astype(np.uint16)


def unstriped(offs):
    return offs[:16].T.reshape(-1).astype(np.int64)


E2M1 = np.array([0.0, 0.5, 1.0, 1.5, 2.0, 3.0, 4.0, 6.0, -0.0, -0.5, -1.0, -1.5, -2.0, -3.0, -4.0, -6.0])


def pack_weight(w, fmt):
    k, n = w.shape
    w = f64(np.asarray(w, np.float32).astype(ml_dtypes.bfloat16)).reshape(k // 32, 32, n)
    amax = np.abs(w).max(1)
    if fmt in ("e4m3", "e5m2"):
        byte = np.frexp(amax)[1] - 1 + 127 - (7 if fmt == "e4m3" else 14)
    else:
        mant, ex = np.frexp(amax / 6.0)
        byte = np.where(mant > 0.5, ex, ex - 1) + 127
    byte = np.clip(np.where(amax > 0, byte, 1), 1, 254)
    scaled = (w * np.exp2(127.0 - byte)[:, None, :]).reshape(k, n).astype(np.float32)
    by_word = np.ascontiguousarray(scaled.reshape(k // 512, 128, 4, n).transpose(0, 1, 3, 2))
    if fmt in ("e4m3", "e5m2"):
        words = by_word.astype(ml_dtypes.float8_e4m3fn if fmt == "e4m3" else ml_dtypes.float8_e5m2).view(np.uint8)
    else:
        c = by_word.astype(ml_dtypes.float4_e2m1fn).view(np.uint8) & 0xF
        words = (c[..., 0::2] | (c[..., 1::2] << 4)).reshape(k // 512, 128, 2 * n)
    return np.ascontiguousarray(words), np.ascontiguousarray(byte.astype(np.uint8).reshape(k // 512, 16, n))


def unpack_weight(words, scales, fmt):
    g, _, n = scales.shape
    words = np.ascontiguousarray(words).reshape(g, 128, n, -1)
    if fmt in ("e4m3", "e5m2"):
        vals = words.view(ml_dtypes.float8_e4m3fn if fmt == "e4m3" else ml_dtypes.float8_e5m2).astype(np.float64)
    else:
        nib = np.empty((g, 128, n, 4), np.uint8)
        nib[..., 0::2] = words & 0xF
        nib[..., 1::2] = words >> 4
        vals = E2M1[nib]
    vals = vals * np.repeat(np.exp2(scales.astype(np.float64) - 127.0), 8, axis=1)[..., None]
    return vals.transpose(0, 1, 3, 2).reshape(g * 512, n)


K, T, J, R, F, Z, C, O, N, E = 512, 1024, 256, 512, 512, 1024, 512, 128, 256, 1024


def setup_inputs():
    n = np.random.standard_normal
    idx = np.random.permutation(T)[:J]
    idx2 = np.random.permutation(Z)[:J]
    idx3 = np.random.permutation(C)[:J]
    idx4 = np.random.permutation(C)[:O]
    idx5 = np.random.permutation(C)[:O]
    idx6 = np.random.permutation(J)[:O]
    idx7 = np.random.permutation(E)[:O]
    fk = mx_kscale(K)
    ff = mx_kscale(F)
    fr = mx_kscale(R)
    xtp = pack_weight(n((K, T)) / fk[:, None], "e4m3")
    xop = pack_weight(n((F, Z)) / ff[:, None], "e2m1")
    wp = pack_weight(n((K, R)) * 1 / np.sqrt(K) * fk[:, None] * fr, "e2m1")
    w2p = pack_weight(n((F, R)) * 1 / np.sqrt(F) * ff[:, None], "e5m2")
    wbp = pack_weight(n((R, N)) * 1 / np.sqrt(R) / fr[:, None], "e5m2")
    return {
        "xt_words": xtp[0],
        "xt_scales": xtp[1],
        "xo_words": xop[0],
        "xo_scales": xop[1],
        "w_words": wp[0],
        "w_scales": wp[1],
        "w2_words": w2p[0],
        "w2_scales": w2p[1],
        "wb_words": wbp[0],
        "wb_scales": wbp[1],
        "offs": striped(idx),
        "offs2": striped(idx2),
        "offs3": striped(idx3),
        "offs4": striped(idx4),
        "offs5": striped(idx5),
        "offs6": striped(idx6),
        "offs7": striped(idx7),
    }


def reference(xt_words, xt_scales, xo_words, xo_scales, w_words, w_scales, w2_words, w2_scales, wb_words, wb_scales, offs, offs2, offs3, offs4, offs5, offs6, offs7):
    idx = unstriped(offs)
    idx2 = unstriped(offs2)
    idx3 = unstriped(offs3)
    idx4 = unstriped(offs4)
    idx5 = unstriped(offs5)
    idx6 = unstriped(offs6)
    idx7 = unstriped(offs7)
    xtu = unpack_weight(xt_words, xt_scales, "e4m3")
    xou = unpack_weight(xo_words, xo_scales, "e2m1")
    wu = unpack_weight(w_words, w_scales, "e2m1")
    w2u = unpack_weight(w2_words, w2_scales, "e5m2")
    wbu = unpack_weight(wb_words, wb_scales, "e5m2")
    xtidxg = xtu[:, idx]
    a = wu.T @ xtidxg
    xoidx2g = xou[:, idx2]
    b = w2u.T @ xoidx2g
    lb = b[:, 0:1]
    lb2 = b[:, 128:129]
    la = a[:, 0:1]
    pw = np.zeros((R, C))
    pw[:, idx3] = a
    hid = np.maximum(pw[:, idx4] * lb, pw[:, idx5] * lb2) - b[:, idx6] * la
    hidq = mxq(hid, 0, "e4m3")
    p = wbu.T @ hidq
    y = np.zeros((N, E))
    y[:, idx7] = p
    return y

@@ -1,0 +1,197 @@
+from contextlib import ExitStack
+
+import concourse.mybir as mybir
+
+K, T, J, R, F, Z, C, O, N, E = 512, 1024, 256, 512, 512, 1024, 512, 128, 256, 1024
+FLOPS = 2 * (K * R * J + F * R * J + R * N * O)
+
+F32 = mybir.dt.float32
+BF16 = mybir.dt.bfloat16
+I32 = mybir.dt.int32
+U32 = mybir.dt.uint32
+U16 = mybir.dt.uint16
+U8 = mybir.dt.uint8
+E4M3 = mybir.dt.float8_e4m3fn_x4
+E5M2 = mybir.dt.float8_e5m2_x4
+E2M1 = mybir.dt.float4_e2m1fn_x4
+COPY = mybir.ActivationFunctionType.Copy
+MAX = mybir.AluOpType.max
+SUB = mybir.AluOpType.subtract
+
+P = 128
+PACK = 4
+
+
+def tile_list_leadreads_twotab_one_scattered_kernel(
+    tc, xt_words, xt_scales, xo_words, xo_scales, w_words, w_scales, w2_words, w2_scales,
+    wb_words, wb_scales, offs, offs2, offs3, offs4, offs5, offs6, offs7, out,
+):
+    nc = tc.nc
+    with ExitStack() as ctx:
+        lists = ctx.enter_context(tc.tile_pool(name="lists", bufs=1))
+        sb = ctx.enter_context(tc.tile_pool(name="sb", bufs=1))
+        shared = ctx.enter_context(tc.tile_pool(name="shared", bufs=1))
+        psum = ctx.enter_context(tc.psum_pool(name="psum", bufs=1))
+
+        def load_list(src, name):
+            t = lists.tile(list(src.shape), U16, name=name)
+            nc.sync.dma_start(t[:], src)
+            return t
+
+        def zeroed_plane(width, name, tag=None):
+            t = sb.tile([P, width], U8, name=name, tag=tag or name, align_bytes=64)
+            nc.vector.memset(t[:].bitcast(I32), 0)
+            return t
+
+        def load_plane(queue, t, src):
+            for q in range(4):
+                queue.dma_start(t[32 * q : 32 * q + 4, :].bitcast(I32), src[0, 4 * q : 4 * q + 4, :].bitcast(I32))
+
+        def load_stage(queue, src, name):
+            t = sb.tile([4, 4, R // 4], I32, name=name, align_bytes=64)
+            queue.dma_start(t[:], src[0].bitcast(I32).rearrange("(q r) c -> r q c", r=4))
+            return t
+
+        def dealt_plane(plane, stage, name):
+            for q in range(4):
+                nc.vector.tensor_copy(plane[32 * q : 32 * q + 4, :].bitcast(I32), stage[:, q, :])
+            t = sb.tile([P, R], U8, name=name, align_bytes=64)
+            nc.vector.tensor_copy(t[:].rearrange("p (t m) -> p t m", t=PACK), plane[:].rearrange("p (m t) -> p t m", t=PACK))
+            return t
+
+        def words32(src):
+            return src[0].rearrange("p n t -> p (n t)").bitcast(I32)
+
+        xt_s = zeroed_plane(T, "xt_s")
+        xo_s = zeroed_plane(Z, "xo_s")
+        w_s = zeroed_plane(R, "w_s")
+        wb_s = zeroed_plane(N, "wb_s")
+
+        l1 = load_list(offs, "l1")
+        w_stage = load_stage(nc.scalar, w_scales, "w_stage")
+        xt_w = shared.tile([P, T], U32, name="xt_w", offset=0, align_bytes=64)
+        nc.sync.dma_start(xt_w[:].bitcast(I32), words32(xt_words))
+        w_w = sb.tile([P, R], U16, name="w_w", align_bytes=64)
+        nc.scalar.dma_start(w_w[:].bitcast(I32), w_words[0].bitcast(I32))
+        load_plane(nc.scalar, xt_s, xt_scales)
+        w2_w = sb.tile([P, R], U32, name="w2_w", align_bytes=64)
+        nc.gpsimd.dma_start(w2_w[:].bitcast(I32), words32(w2_words))
+        w2_stage = load_stage(nc.gpsimd, w2_scales, "w2_stage")
+        l2 = load_list(offs2, "l2")
+        xo_w = shared.tile([P, Z], U16, name="xo_w", offset=5120, align_bytes=64)
+        nc.sync.dma_start(xo_w[:].bitcast(I32), xo_words[0].bitcast(I32))
+        load_plane(nc.sync, xo_s, xo_scales)
+        l3 = load_list(offs3, "l3")
+        l6 = load_list(offs6, "l6")
+        l4 = load_list(offs4, "l4")
+        l5 = load_list(offs5, "l5")
+        l7 = load_list(offs7, "l7")
+        wb_w = sb.tile([P, N], U32, name="wb_w", align_bytes=64)
+        nc.sync.dma_start(wb_w[:].bitcast(I32), words32(wb_words))
+        load_plane(nc.sync, wb_s, wb_scales)
+
+        boards = {}
+        for t in (0, 2):
+            boards[t] = sb.tile([P, C], F32, name=f"board{t}", tag=f"board{t}", align_bytes=64)
+            nc.vector.memset(boards[t][:], 0.0)
+
+        w_sp = dealt_plane(w_s, w_stage, "w_sp")
+        w_wp = sb.tile([P, R], U16, name="w_wp", align_bytes=64)
+        nc.scalar.copy(w_wp[:].rearrange("p (t m) -> p t m", t=PACK), w_w[:].rearrange("p (m t) -> p t m", t=PACK))
+
+        xt_sg = sb.tile([P, J], U8, name="xt_sg", tag="w_s", align_bytes=64)
+        nc.vector.tensor_copy(xt_sg[:], xt_s[:].indirect(l1[:]))
+        xt_wg = sb.tile([P, J], U32, name="xt_wg", tag="xt_s", align_bytes=64)
+        nc.vector.tensor_copy(xt_wg[:], xt_w[:].indirect(l1[:]))
+
+        w2_wp = sb.tile([P, R], U32, name="w2_wp", align_bytes=64)
+        nc.scalar.copy(w2_wp[:].rearrange("p (t m) -> p t m", t=PACK), w2_w[:].rearrange("p (m t) -> p t m", t=PACK))
+        w2_s = shared.tile([P, R], U8, name="w2_s", offset=0, align_bytes=64)
+        nc.vector.memset(w2_s[:].bitcast(I32), 0)
+        w2_sp = dealt_plane(w2_s, w2_stage, "w2_sp")
+
+        a_sb = []
+        for t in range(PACK):
+            acc = psum.tile([P, J], F32, name=f"a_ps{t}", tag=f"bank{t}")
+            cols = slice(t * P, (t + 1) * P)
+            nc.tensor.matmul_mx(out=acc[:], lhsT=w_wp[:, cols].bitcast(E2M1), lhsT_scale=w_sp[:, cols],
+                                rhs=xt_wg[:].bitcast(E4M3), rhs_scale=xt_sg[:], start=True, stop=True)
+            at = sb.tile([P, J], F32, name=f"a{t}")
+            nc.scalar.copy(at[:], acc[:])
+            a_sb.append(at)
+
+        xo_sg = shared.tile([P, J], U8, name="xo_sg", offset=512, align_bytes=64)
+        nc.vector.tensor_copy(xo_sg[:], xo_s[:].indirect(l2[:]))
+        xo_wg = sb.tile([P, J], U16, name="xo_wg", tag="xo_s", align_bytes=64)
+        nc.vector.tensor_copy(xo_wg[:], xo_w[:].indirect(l2[:]))
+
+        for t in (1, 3):
+            boards[t] = shared.tile([P, C], F32, name=f"board{t}", offset=4096 + 1024 * (t - 1), align_bytes=64)
+            nc.gpsimd.memset(boards[t][:], 0.0)
+        nc.scalar.activation(boards[2][:].indirect(l3[:]), a_sb[2][:], COPY)
+        nc.vector.tensor_copy(boards[0][:].indirect(l3[:]), a_sb[0][:])
+
+        b_sb = {}
+        for t in (2, 3, 0, 1):
+            acc = psum.tile([P, J], F32, name=f"b_ps{t}", tag=f"bank{PACK + t}")
+            cols = slice(t * P, (t + 1) * P)
+            nc.tensor.matmul_mx(out=acc[:], lhsT=w2_wp[:, cols].bitcast(E5M2), lhsT_scale=w2_sp[:, cols],
+                                rhs=xo_wg[:].bitcast(E2M1), rhs_scale=xo_sg[:], start=True, stop=True)
+            bt = sb.tile([P, J], F32, name=f"b{t}")
+            if t != 3:
+                nc.scalar.copy(bt[:], acc[:])
+            else:
+                nc.vector.tensor_copy(bt[:], acc[:])
+            b_sb[t] = bt
+
+        for t in (1, 3):
+            nc.vector.tensor_copy(boards[t][:].indirect(l3[:]), a_sb[t][:])
+
+        g4 = sb.tile([P, PACK, O], F32, name="g4")
+        g5 = sb.tile([P, PACK, O], F32, name="g5")
+        g6 = sb.tile([P, PACK, O], F32, name="g6")
+        def slot_look(t):
+            nc.scalar.activation(g6[:, t, :], b_sb[t][:].indirect(l6[:]), COPY, scale=a_sb[t][:, 0:1])
+
+        def board_looks(t):
+            nc.scalar.activation(g4[:, t, :], boards[t][:].indirect(l4[:]), COPY, scale=b_sb[t][:, 0:1])
+            nc.scalar.activation(g5[:, t, :], boards[t][:].indirect(l5[:]), COPY, scale=b_sb[t][:, 128:129])
+
+        for t in (2, 0):
+            slot_look(t)
+            board_looks(t)
+        for t in (1, 3):
+            slot_look(t)
+        for t in (1, 3):
+            board_looks(t)
+
+        pages = []
+        for h, old in enumerate((2, 0)):
+            pg = sb.tile([P, E], F32, name=f"page{h}", tag=f"board{old}", align_bytes=64)
+            nc.gpsimd.memset(pg[:], 0.0)
+            pages.append(pg)
+
+        larger = sb.tile([P, PACK, O], F32, name="larger")
+        hid = sb.tile([P, O, PACK], BF16, name="hid", align_bytes=64)
+        for lo, hi in ((0, 3), (3, 4)):
+            nc.vector.tensor_tensor(larger[:, lo:hi, :], g4[:, lo:hi, :], g5[:, lo:hi, :], MAX)
+            nc.vector.tensor_tensor(hid[:, :, lo:hi], larger[:, lo:hi, :].rearrange("p t o -> p o t"),
+                                    g6[:, lo:hi, :].rearrange("p t o -> p o t"), SUB)
+        hid_w = sb.tile([P, O], U32, name="hid_w", align_bytes=64)
+        hid_s = sb.tile([P, O], U8, name="hid_s", align_bytes=64)
+        nc.vector.quantize_mx(out=hid_w[:].bitcast(E4M3), scales=hid_s[:], in_=hid[:].rearrange("p o t -> p (o t)"))
+
+        for h in range(N // P):
+            acc = psum.tile([P, O], F32, name=f"p_ps{h}", tag=f"bank{h}")
+            cols = slice(h * P, (h + 1) * P)
+            nc.tensor.matmul_mx(out=acc[:], lhsT=wb_w[:, cols].bitcast(E5M2), lhsT_scale=wb_s[:, cols],
+                                rhs=hid_w[:].bitcast(E4M3), rhs_scale=hid_s[:], start=True, stop=True)
+            pt = sb.tile([P, O], F32, name=f"p{h}")
+            if h == 0:
+                nc.vector.tensor_copy(pt[:], acc[:])
+                nc.vector.tensor_copy(pages[h][:].indirect(l7[:]), pt[:])
+                nc.sync.dma_start(out[h * P : (h + 1) * P, :], pages[h][:])
+            else:
+                nc.scalar.copy(pt[:], acc[:])
+                nc.scalar.activation(pages[h][:].indirect(l7[:]), pt[:], COPY)
+                nc.scalar.dma_start(out[h * P : (h + 1) * P, :], pages[h][:])

@@ -43,8 +43,8 @@ def tile_list_leadreads_twotab_one_scattered_kernel(
             nc.vector.memset(t[:].bitcast(I32), 0)
             return t
 
-        def load_plane(queue, t, src):
-            for q in range(4):
+        def load_plane(queue, t, src, quadrants=range(4)):
+            for q in quadrants:
                 queue.dma_start(t[32 * q : 32 * q + 4, :].bitcast(I32), src[0, 4 * q : 4 * q + 4, :].bitcast(I32))
 
         def load_stage(queue, src, name):
@@ -52,11 +52,9 @@ def tile_list_leadreads_twotab_one_scattered_kernel(
             queue.dma_start(t[:], src[0].bitcast(I32).rearrange("(q r) c -> r q c", r=4))
             return t
 
-        def dealt_plane(plane, stage, name):
-            for q in range(4):
-                nc.vector.tensor_copy(plane[32 * q : 32 * q + 4, :].bitcast(I32), stage[:, q, :])
+        def dealt_plane(plane, name):
             t = sb.tile([P, R], U8, name=name, align_bytes=64)
-            nc.vector.tensor_copy(t[:].rearrange("p (t m) -> p t m", t=PACK), plane[:].rearrange("p (m t) -> p t m", t=PACK))
+            nc.vector.tensor_copy(t[:].rearrange("p (t m) -> p m t", t=PACK), plane[:].rearrange("p (m t) -> p m t", t=PACK))
             return t
 
         def words32(src):
@@ -64,51 +62,53 @@ def tile_list_leadreads_twotab_one_scattered_kernel(
 
         xt_s = zeroed_plane(T, "xt_s")
         xo_s = zeroed_plane(Z, "xo_s")
+        w2_s = zeroed_plane(R, "w2_s")
         w_s = zeroed_plane(R, "w_s")
-        wb_s = zeroed_plane(N, "wb_s")
 
         l1 = load_list(offs, "l1")
         w_stage = load_stage(nc.scalar, w_scales, "w_stage")
         xt_w = shared.tile([P, T], U32, name="xt_w", offset=0, align_bytes=64)
         nc.sync.dma_start(xt_w[:].bitcast(I32), words32(xt_words))
         w_w = sb.tile([P, R], U16, name="w_w", align_bytes=64)
-        nc.scalar.dma_start(w_w[:].bitcast(I32), w_words[0].bitcast(I32))
-        load_plane(nc.scalar, xt_s, xt_scales)
-        w2_w = sb.tile([P, R], U32, name="w2_w", align_bytes=64)
-        nc.gpsimd.dma_start(w2_w[:].bitcast(I32), words32(w2_words))
-        w2_stage = load_stage(nc.gpsimd, w2_scales, "w2_stage")
-        l2 = load_list(offs2, "l2")
-        xo_w = shared.tile([P, Z], U16, name="xo_w", offset=5120, align_bytes=64)
+        nc.sync.dma_start(w_w[:].bitcast(I32), w_words[0].bitcast(I32))
+        load_plane(nc.sync, xt_s, xt_scales)
+        xo_w = sb.tile([P, Z], U16, name="xo_w", align_bytes=64)
         nc.sync.dma_start(xo_w[:].bitcast(I32), xo_words[0].bitcast(I32))
+        w2_w = sb.tile([P, R], U32, name="w2_w", align_bytes=64)
+        nc.sync.dma_start(w2_w[:].bitcast(I32), words32(w2_words))
+        l2 = load_list(offs2, "l2")
         load_plane(nc.sync, xo_s, xo_scales)
+        load_plane(nc.gpsimd, w2_s, w2_scales, (0, 1))
+        load_plane(nc.sync, w2_s, w2_scales, (2, 3))
         l3 = load_list(offs3, "l3")
-        l6 = load_list(offs6, "l6")
         l4 = load_list(offs4, "l4")
         l5 = load_list(offs5, "l5")
+        l6 = load_list(offs6, "l6")
         l7 = load_list(offs7, "l7")
         wb_w = sb.tile([P, N], U32, name="wb_w", align_bytes=64)
         nc.sync.dma_start(wb_w[:].bitcast(I32), words32(wb_words))
-        load_plane(nc.sync, wb_s, wb_scales)
 
         boards = {}
-        for t in (0, 2):
+        for t in (0, 2, 1):
             boards[t] = sb.tile([P, C], F32, name=f"board{t}", tag=f"board{t}", align_bytes=64)
             nc.vector.memset(boards[t][:], 0.0)
+        wb_s = zeroed_plane(N, "wb_s")
+        load_plane(nc.sync, wb_s, wb_scales)
 
-        w_sp = dealt_plane(w_s, w_stage, "w_sp")
+        for q in range(4):
+            nc.vector.tensor_copy(w_s[32 * q : 32 * q + 4, :].bitcast(I32), w_stage[:, q, :])
+        w_sp = dealt_plane(w_s, "w_sp")
         w_wp = sb.tile([P, R], U16, name="w_wp", align_bytes=64)
-        nc.scalar.copy(w_wp[:].rearrange("p (t m) -> p t m", t=PACK), w_w[:].rearrange("p (m t) -> p t m", t=PACK))
+        nc.scalar.copy(w_wp[:].rearrange("p (t m) -> p m t", t=PACK), w_w[:].rearrange("p (m t) -> p m t", t=PACK))
+
+        w2_wp = sb.tile([P, R], U32, name="w2_wp", align_bytes=64)
+        nc.scalar.copy(w2_wp[:].rearrange("p (t m) -> p m t", t=PACK), w2_w[:].rearrange("p (m t) -> p m t", t=PACK))
 
         xt_sg = sb.tile([P, J], U8, name="xt_sg", tag="w_s", align_bytes=64)
         nc.vector.tensor_copy(xt_sg[:], xt_s[:].indirect(l1[:]))
         xt_wg = sb.tile([P, J], U32, name="xt_wg", tag="xt_s", align_bytes=64)
         nc.vector.tensor_copy(xt_wg[:], xt_w[:].indirect(l1[:]))
 
-        w2_wp = sb.tile([P, R], U32, name="w2_wp", align_bytes=64)
-        nc.scalar.copy(w2_wp[:].rearrange("p (t m) -> p t m", t=PACK), w2_w[:].rearrange("p (m t) -> p t m", t=PACK))
-        w2_s = shared.tile([P, R], U8, name="w2_s", offset=0, align_bytes=64)
-        nc.vector.memset(w2_s[:].bitcast(I32), 0)
-        w2_sp = dealt_plane(w2_s, w2_stage, "w2_sp")
 
         a_sb = []
         for t in range(PACK):
@@ -120,63 +120,63 @@ def tile_list_leadreads_twotab_one_scattered_kernel(
             nc.scalar.copy(at[:], acc[:])
             a_sb.append(at)
 
+        xo_wg = shared.tile([P, J], U16, name="xo_wg", offset=0, align_bytes=64)
+        nc.vector.tensor_copy(xo_wg[:], xo_w[:].indirect(l2[:]))
         xo_sg = shared.tile([P, J], U8, name="xo_sg", offset=512, align_bytes=64)
         nc.vector.tensor_copy(xo_sg[:], xo_s[:].indirect(l2[:]))
-        xo_wg = sb.tile([P, J], U16, name="xo_wg", tag="xo_s", align_bytes=64)
-        nc.vector.tensor_copy(xo_wg[:], xo_w[:].indirect(l2[:]))
+        w2_sp = dealt_plane(w2_s, "w2_sp")
 
-        for t in (1, 3):
-            boards[t] = shared.tile([P, C], F32, name=f"board{t}", offset=4096 + 1024 * (t - 1), align_bytes=64)
-            nc.gpsimd.memset(boards[t][:], 0.0)
         nc.scalar.activation(boards[2][:].indirect(l3[:]), a_sb[2][:], COPY)
-        nc.vector.tensor_copy(boards[0][:].indirect(l3[:]), a_sb[0][:])
+        for t in (0, 1):
+            nc.vector.tensor_copy(boards[t][:].indirect(l3[:]), a_sb[t][:])
 
         b_sb = {}
-        for t in (2, 3, 0, 1):
+        for t in (2, 0, 1, 3):
             acc = psum.tile([P, J], F32, name=f"b_ps{t}", tag=f"bank{PACK + t}")
             cols = slice(t * P, (t + 1) * P)
             nc.tensor.matmul_mx(out=acc[:], lhsT=w2_wp[:, cols].bitcast(E5M2), lhsT_scale=w2_sp[:, cols],
                                 rhs=xo_wg[:].bitcast(E2M1), rhs_scale=xo_sg[:], start=True, stop=True)
             bt = sb.tile([P, J], F32, name=f"b{t}")
-            if t != 3:
+            if t % 2 == 0:
                 nc.scalar.copy(bt[:], acc[:])
             else:
                 nc.vector.tensor_copy(bt[:], acc[:])
             b_sb[t] = bt
 
-        for t in (1, 3):
-            nc.vector.tensor_copy(boards[t][:].indirect(l3[:]), a_sb[t][:])
+        boards[3] = sb.tile([P, C], F32, name="board3", tag="w2_sp", align_bytes=64)
+        nc.gpsimd.memset(boards[3][:], 0.0)
+        pages = [sb.tile([P, E], F32, name="page0", tag="w2_wp", align_bytes=64),
+                 shared.tile([P, E], F32, name="page1", offset=0, align_bytes=64)]
+        for pg in pages:
+            nc.gpsimd.memset(pg[:], 0.0)
+        nc.vector.tensor_copy(boards[3][:].indirect(l3[:]), a_sb[3][:])
 
-        g4 = sb.tile([P, PACK, O], F32, name="g4")
-        g5 = sb.tile([P, PACK, O], F32, name="g5")
-        g6 = sb.tile([P, PACK, O], F32, name="g6")
+        groups = ((0, 3), (3, 4))
+        looks = {}
+        for lo, hi in groups:
+            for name in ("g4", "g5", "g6", "larger"):
+                looks[name, lo] = sb.tile([P, hi - lo, O], F32, name=f"{name}_{lo}")
+
         def slot_look(t):
-            nc.scalar.activation(g6[:, t, :], b_sb[t][:].indirect(l6[:]), COPY, scale=a_sb[t][:, 0:1])
+            lo = t // 3 * 3
+            nc.scalar.activation(looks["g6", lo][:, t - lo, :], b_sb[t][:].indirect(l6[:]), COPY, scale=a_sb[t][:, 0:1])
 
         def board_looks(t):
-            nc.scalar.activation(g4[:, t, :], boards[t][:].indirect(l4[:]), COPY, scale=b_sb[t][:, 0:1])
-            nc.scalar.activation(g5[:, t, :], boards[t][:].indirect(l5[:]), COPY, scale=b_sb[t][:, 128:129])
+            lo = t // 3 * 3
+            nc.scalar.activation(looks["g4", lo][:, t - lo, :], boards[t][:].indirect(l4[:]), COPY, scale=b_sb[t][:, 0:1])
+            nc.scalar.activation(looks["g5", lo][:, t - lo, :], boards[t][:].indirect(l5[:]), COPY, scale=b_sb[t][:, 128:129])
 
-        for t in (2, 0):
-            slot_look(t)
+        for t in (2, 0, 1):
             board_looks(t)
-        for t in (1, 3):
             slot_look(t)
-        for t in (1, 3):
-            board_looks(t)
+        board_looks(3)
+        slot_look(3)
 
-        pages = []
-        for h, old in enumerate((2, 0)):
-            pg = sb.tile([P, E], F32, name=f"page{h}", tag=f"board{old}", align_bytes=64)
-            nc.gpsimd.memset(pg[:], 0.0)
-            pages.append(pg)
-
-        larger = sb.tile([P, PACK, O], F32, name="larger")
         hid = sb.tile([P, O, PACK], BF16, name="hid", align_bytes=64)
-        for lo, hi in ((0, 3), (3, 4)):
-            nc.vector.tensor_tensor(larger[:, lo:hi, :], g4[:, lo:hi, :], g5[:, lo:hi, :], MAX)
-            nc.vector.tensor_tensor(hid[:, :, lo:hi], larger[:, lo:hi, :].rearrange("p t o -> p o t"),
-                                    g6[:, lo:hi, :].rearrange("p t o -> p o t"), SUB)
+        for lo, hi in groups:
+            nc.vector.tensor_tensor(looks["larger", lo][:], looks["g4", lo][:], looks["g5", lo][:], MAX)
+            nc.vector.tensor_tensor(hid[:, :, lo:hi], looks["larger", lo][:].rearrange("p t o -> p o t"),
+                                    looks["g6", lo][:].rearrange("p t o -> p o t"), SUB)
         hid_w = sb.tile([P, O], U32, name="hid_w", align_bytes=64)
         hid_s = sb.tile([P, O], U8, name="hid_s", align_bytes=64)
         nc.vector.quantize_mx(out=hid_w[:].bitcast(E4M3), scales=hid_s[:], in_=hid[:].rearrange("p o t -> p (o t)"))

@@ -60,23 +60,24 @@ def tile_list_leadreads_twotab_one_scattered_kernel(
         def words32(src):
             return src[0].rearrange("p n t -> p (n t)").bitcast(I32)
 
-        xt_s = zeroed_plane(T, "xt_s")
+        xt_s = shared.tile([P, T], U8, name="xt_s", offset=0, align_bytes=64)
+        nc.vector.memset(xt_s[:].bitcast(I32), 0)
         xo_s = zeroed_plane(Z, "xo_s")
         w2_s = zeroed_plane(R, "w2_s")
         w_s = zeroed_plane(R, "w_s")
 
         l1 = load_list(offs, "l1")
         w_stage = load_stage(nc.scalar, w_scales, "w_stage")
-        xt_w = shared.tile([P, T], U32, name="xt_w", offset=0, align_bytes=64)
+        l2 = load_list(offs2, "l2")
+        xt_w = sb.tile([P, T], U32, name="xt_w", align_bytes=64)
         nc.sync.dma_start(xt_w[:].bitcast(I32), words32(xt_words))
         w_w = sb.tile([P, R], U16, name="w_w", align_bytes=64)
         nc.sync.dma_start(w_w[:].bitcast(I32), w_words[0].bitcast(I32))
         load_plane(nc.sync, xt_s, xt_scales)
-        xo_w = sb.tile([P, Z], U16, name="xo_w", align_bytes=64)
-        nc.sync.dma_start(xo_w[:].bitcast(I32), xo_words[0].bitcast(I32))
         w2_w = sb.tile([P, R], U32, name="w2_w", align_bytes=64)
         nc.sync.dma_start(w2_w[:].bitcast(I32), words32(w2_words))
-        l2 = load_list(offs2, "l2")
+        xo_w = sb.tile([P, Z], U16, name="xo_w", align_bytes=64)
+        nc.sync.dma_start(xo_w[:].bitcast(I32), xo_words[0].bitcast(I32))
         load_plane(nc.sync, xo_s, xo_scales)
         load_plane(nc.gpsimd, w2_s, w2_scales, (0, 1))
         load_plane(nc.sync, w2_s, w2_scales, (2, 3))
@@ -104,21 +105,20 @@ def tile_list_leadreads_twotab_one_scattered_kernel(
         w2_wp = sb.tile([P, R], U32, name="w2_wp", align_bytes=64)
         nc.scalar.copy(w2_wp[:].rearrange("p (t m) -> p m t", t=PACK), w2_w[:].rearrange("p (m t) -> p m t", t=PACK))
 
-        xt_sg = sb.tile([P, J], U8, name="xt_sg", tag="w_s", align_bytes=64)
-        nc.vector.tensor_copy(xt_sg[:], xt_s[:].indirect(l1[:]))
-        xt_wg = sb.tile([P, J], U32, name="xt_wg", tag="xt_s", align_bytes=64)
+        xt_wg = sb.tile([P, J], U32, name="xt_wg", align_bytes=64)
         nc.vector.tensor_copy(xt_wg[:], xt_w[:].indirect(l1[:]))
+        xt_sg = sb.tile([P, J], U8, name="xt_sg", align_bytes=64)
+        nc.vector.tensor_copy(xt_sg[:], xt_s[:].indirect(l1[:]))
 
-
-        a_sb = []
-        for t in range(PACK):
+        a_sb = {}
+        for t in (0, 2, 1, 3):
             acc = psum.tile([P, J], F32, name=f"a_ps{t}", tag=f"bank{t}")
             cols = slice(t * P, (t + 1) * P)
             nc.tensor.matmul_mx(out=acc[:], lhsT=w_wp[:, cols].bitcast(E2M1), lhsT_scale=w_sp[:, cols],
                                 rhs=xt_wg[:].bitcast(E4M3), rhs_scale=xt_sg[:], start=True, stop=True)
             at = sb.tile([P, J], F32, name=f"a{t}")
             nc.scalar.copy(at[:], acc[:])
-            a_sb.append(at)
+            a_sb[t] = at
 
         xo_wg = shared.tile([P, J], U16, name="xo_wg", offset=0, align_bytes=64)
         nc.vector.tensor_copy(xo_wg[:], xo_w[:].indirect(l2[:]))
@@ -154,7 +154,7 @@ def tile_list_leadreads_twotab_one_scattered_kernel(
         groups = ((0, 3), (3, 4))
         looks = {}
         for lo, hi in groups:
-            for name in ("g4", "g5", "g6", "larger"):
+            for name in ("g4", "g5", "g6"):
                 looks[name, lo] = sb.tile([P, hi - lo, O], F32, name=f"{name}_{lo}")
 
         def slot_look(t):
@@ -174,8 +174,9 @@ def tile_list_leadreads_twotab_one_scattered_kernel(
 
         hid = sb.tile([P, O, PACK], BF16, name="hid", align_bytes=64)
         for lo, hi in groups:
-            nc.vector.tensor_tensor(looks["larger", lo][:], looks["g4", lo][:], looks["g5", lo][:], MAX)
-            nc.vector.tensor_tensor(hid[:, :, lo:hi], looks["larger", lo][:].rearrange("p t o -> p o t"),
+            larger = sb.tile([P, hi - lo, O], F32, name=f"larger{lo}", tag="larger")
+            nc.vector.tensor_tensor(larger[:], looks["g4", lo][:], looks["g5", lo][:], MAX)
+            nc.vector.tensor_tensor(hid[:, :, lo:hi], larger[:].rearrange("p t o -> p o t"),
                                     looks["g6", lo][:].rearrange("p t o -> p o t"), SUB)
         hid_w = sb.tile([P, O], U32, name="hid_w", align_bytes=64)
         hid_s = sb.tile([P, O], U8, name="hid_s", align_bytes=64)

@@ -60,7 +60,7 @@ def tile_list_leadreads_twotab_one_scattered_kernel(
         def words32(src):
             return src[0].rearrange("p n t -> p (n t)").bitcast(I32)
 
-        xt_s = shared.tile([P, T], U8, name="xt_s", offset=0, align_bytes=64)
+        xt_s = shared.tile([P, T], U8, name="xt_s", offset=3584, align_bytes=64)
         nc.vector.memset(xt_s[:].bitcast(I32), 0)
         xo_s = zeroed_plane(Z, "xo_s")
         w2_s = zeroed_plane(R, "w2_s")
@@ -74,13 +74,12 @@ def tile_list_leadreads_twotab_one_scattered_kernel(
         w_w = sb.tile([P, R], U16, name="w_w", align_bytes=64)
         nc.sync.dma_start(w_w[:].bitcast(I32), w_words[0].bitcast(I32))
         load_plane(nc.sync, xt_s, xt_scales)
-        w2_w = sb.tile([P, R], U32, name="w2_w", align_bytes=64)
-        nc.sync.dma_start(w2_w[:].bitcast(I32), words32(w2_words))
         xo_w = sb.tile([P, Z], U16, name="xo_w", align_bytes=64)
-        nc.sync.dma_start(xo_w[:].bitcast(I32), xo_words[0].bitcast(I32))
+        nc.gpsimd.dma_start(xo_w[:].bitcast(I32), xo_words[0].bitcast(I32))
+        w2_w = sb.tile([P, R], U32, name="w2_w", align_bytes=64)
+        nc.gpsimd.dma_start(w2_w[:].bitcast(I32), words32(w2_words))
         load_plane(nc.sync, xo_s, xo_scales)
-        load_plane(nc.gpsimd, w2_s, w2_scales, (0, 1))
-        load_plane(nc.sync, w2_s, w2_scales, (2, 3))
+        load_plane(nc.sync, w2_s, w2_scales)
         l3 = load_list(offs3, "l3")
         l4 = load_list(offs4, "l4")
         l5 = load_list(offs5, "l5")
@@ -102,9 +101,6 @@ def tile_list_leadreads_twotab_one_scattered_kernel(
         w_wp = sb.tile([P, R], U16, name="w_wp", align_bytes=64)
         nc.scalar.copy(w_wp[:].rearrange("p (t m) -> p m t", t=PACK), w_w[:].rearrange("p (m t) -> p m t", t=PACK))
 
-        w2_wp = sb.tile([P, R], U32, name="w2_wp", align_bytes=64)
-        nc.scalar.copy(w2_wp[:].rearrange("p (t m) -> p m t", t=PACK), w2_w[:].rearrange("p (m t) -> p m t", t=PACK))
-
         xt_wg = sb.tile([P, J], U32, name="xt_wg", align_bytes=64)
         nc.vector.tensor_copy(xt_wg[:], xt_w[:].indirect(l1[:]))
         xt_sg = sb.tile([P, J], U8, name="xt_sg", align_bytes=64)
@@ -120,9 +116,11 @@ def tile_list_leadreads_twotab_one_scattered_kernel(
             nc.scalar.copy(at[:], acc[:])
             a_sb[t] = at
 
-        xo_wg = shared.tile([P, J], U16, name="xo_wg", offset=0, align_bytes=64)
+        xo_wg = shared.tile([P, J], U16, name="xo_wg", offset=3584, align_bytes=64)
         nc.vector.tensor_copy(xo_wg[:], xo_w[:].indirect(l2[:]))
-        xo_sg = shared.tile([P, J], U8, name="xo_sg", offset=512, align_bytes=64)
+        w2_wp = shared.tile([P, R], U32, name="w2_wp", offset=4352, align_bytes=64)
+        nc.vector.tensor_copy(w2_wp[:].rearrange("p (t m) -> p m t", t=PACK), w2_w[:].rearrange("p (m t) -> p m t", t=PACK))
+        xo_sg = shared.tile([P, J], U8, name="xo_sg", offset=4096, align_bytes=64)
         nc.vector.tensor_copy(xo_sg[:], xo_s[:].indirect(l2[:]))
         w2_sp = dealt_plane(w2_s, "w2_sp")
 
@@ -145,7 +143,7 @@ def tile_list_leadreads_twotab_one_scattered_kernel(
 
         boards[3] = sb.tile([P, C], F32, name="board3", tag="w2_sp", align_bytes=64)
         nc.gpsimd.memset(boards[3][:], 0.0)
-        pages = [sb.tile([P, E], F32, name="page0", tag="w2_wp", align_bytes=64),
+        pages = [shared.tile([P, E], F32, name="page0", offset=4096, align_bytes=64),
                  shared.tile([P, E], F32, name="page1", offset=0, align_bytes=64)]
         for pg in pages:
             nc.gpsimd.memset(pg[:], 0.0)

@@ -63,7 +63,8 @@ def tile_list_leadreads_twotab_one_scattered_kernel(
         xt_s = shared.tile([P, T], U8, name="xt_s", offset=3584, align_bytes=64)
         nc.vector.memset(xt_s[:].bitcast(I32), 0)
         xo_s = zeroed_plane(Z, "xo_s")
-        w2_s = zeroed_plane(R, "w2_s")
+        w2_s = shared.tile([P, R], U8, name="w2_s", offset=8960, align_bytes=64)
+        nc.vector.memset(w2_s[:].bitcast(I32), 0)
         w_s = zeroed_plane(R, "w_s")
 
         l1 = load_list(offs, "l1")
@@ -74,13 +75,13 @@ def tile_list_leadreads_twotab_one_scattered_kernel(
         w_w = sb.tile([P, R], U16, name="w_w", align_bytes=64)
         nc.sync.dma_start(w_w[:].bitcast(I32), w_words[0].bitcast(I32))
         load_plane(nc.sync, xt_s, xt_scales)
+        l3 = load_list(offs3, "l3")
         xo_w = sb.tile([P, Z], U16, name="xo_w", align_bytes=64)
         nc.gpsimd.dma_start(xo_w[:].bitcast(I32), xo_words[0].bitcast(I32))
         w2_w = sb.tile([P, R], U32, name="w2_w", align_bytes=64)
         nc.gpsimd.dma_start(w2_w[:].bitcast(I32), words32(w2_words))
         load_plane(nc.sync, xo_s, xo_scales)
         load_plane(nc.sync, w2_s, w2_scales)
-        l3 = load_list(offs3, "l3")
         l4 = load_list(offs4, "l4")
         l5 = load_list(offs5, "l5")
         l6 = load_list(offs6, "l6")
@@ -106,16 +107,6 @@ def tile_list_leadreads_twotab_one_scattered_kernel(
         xt_sg = sb.tile([P, J], U8, name="xt_sg", align_bytes=64)
         nc.vector.tensor_copy(xt_sg[:], xt_s[:].indirect(l1[:]))
 
-        a_sb = {}
-        for t in (0, 2, 1, 3):
-            acc = psum.tile([P, J], F32, name=f"a_ps{t}", tag=f"bank{t}")
-            cols = slice(t * P, (t + 1) * P)
-            nc.tensor.matmul_mx(out=acc[:], lhsT=w_wp[:, cols].bitcast(E2M1), lhsT_scale=w_sp[:, cols],
-                                rhs=xt_wg[:].bitcast(E4M3), rhs_scale=xt_sg[:], start=True, stop=True)
-            at = sb.tile([P, J], F32, name=f"a{t}")
-            nc.scalar.copy(at[:], acc[:])
-            a_sb[t] = at
-
         xo_wg = shared.tile([P, J], U16, name="xo_wg", offset=3584, align_bytes=64)
         nc.vector.tensor_copy(xo_wg[:], xo_w[:].indirect(l2[:]))
         w2_wp = shared.tile([P, R], U32, name="w2_wp", offset=4352, align_bytes=64)
@@ -123,6 +114,20 @@ def tile_list_leadreads_twotab_one_scattered_kernel(
         xo_sg = shared.tile([P, J], U8, name="xo_sg", offset=4096, align_bytes=64)
         nc.vector.tensor_copy(xo_sg[:], xo_s[:].indirect(l2[:]))
         w2_sp = dealt_plane(w2_s, "w2_sp")
+
+        a_sb = {}
+        for t in (2, 3, 0, 1):
+            acc = psum.tile([P, J], F32, name=f"a_ps{t}", tag=f"bank{t}")
+            cols = slice(t * P, (t + 1) * P)
+            nc.tensor.matmul_mx(out=acc[:], lhsT=w_wp[:, cols].bitcast(E2M1), lhsT_scale=w_sp[:, cols],
+                                rhs=xt_wg[:].bitcast(E4M3), rhs_scale=xt_sg[:], start=True, stop=True)
+            if t < 2:
+                at = shared.tile([P, J], F32, name=f"a{t}", offset=8192 + 1024 * t, align_bytes=64)
+                nc.vector.tensor_copy(at[:], acc[:])
+            else:
+                at = sb.tile([P, J], F32, name=f"a{t}")
+                nc.scalar.copy(at[:], acc[:])
+            a_sb[t] = at
 
         nc.scalar.activation(boards[2][:].indirect(l3[:]), a_sb[2][:], COPY)
         for t in (0, 1):
@@ -135,10 +140,7 @@ def tile_list_leadreads_twotab_one_scattered_kernel(
             nc.tensor.matmul_mx(out=acc[:], lhsT=w2_wp[:, cols].bitcast(E5M2), lhsT_scale=w2_sp[:, cols],
                                 rhs=xo_wg[:].bitcast(E2M1), rhs_scale=xo_sg[:], start=True, stop=True)
             bt = sb.tile([P, J], F32, name=f"b{t}")
-            if t % 2 == 0:
-                nc.scalar.copy(bt[:], acc[:])
-            else:
-                nc.vector.tensor_copy(bt[:], acc[:])
+            nc.scalar.copy(bt[:], acc[:])
             b_sb[t] = bt
 
         boards[3] = sb.tile([P, C], F32, name="board3", tag="w2_sp", align_bytes=64)

from contextlib import ExitStack

import concourse.mybir as mybir

K, T, J, R, F, Z, C, O, N, E = 512, 1024, 256, 512, 512, 1024, 512, 128, 256, 1024
FLOPS = 2 * (K * R * J + F * R * J + R * N * O)

F32 = mybir.dt.float32
BF16 = mybir.dt.bfloat16
I32 = mybir.dt.int32
U32 = mybir.dt.uint32
U16 = mybir.dt.uint16
U8 = mybir.dt.uint8
E4M3 = mybir.dt.float8_e4m3fn_x4
E5M2 = mybir.dt.float8_e5m2_x4
E2M1 = mybir.dt.float4_e2m1fn_x4
COPY = mybir.ActivationFunctionType.Copy
MAX = mybir.AluOpType.max
SUB = mybir.AluOpType.subtract

P = 128
PACK = 4


def tile_list_leadreads_twotab_one_scattered_kernel(
    tc, xt_words, xt_scales, xo_words, xo_scales, w_words, w_scales, w2_words, w2_scales,
    wb_words, wb_scales, offs, offs2, offs3, offs4, offs5, offs6, offs7, out,
):
    nc = tc.nc
    with ExitStack() as ctx:
        lists = ctx.enter_context(tc.tile_pool(name="lists", bufs=1))
        sb = ctx.enter_context(tc.tile_pool(name="sb", bufs=1))
        shared = ctx.enter_context(tc.tile_pool(name="shared", bufs=1))
        psum = ctx.enter_context(tc.psum_pool(name="psum", bufs=1))

        def load_list(src, name):
            t = lists.tile(list(src.shape), U16, name=name)
            nc.sync.dma_start(t[:], src)
            return t

        def zeroed_plane(width, name, tag=None):
            t = sb.tile([P, width], U8, name=name, tag=tag or name, align_bytes=64)
            nc.vector.memset(t[:].bitcast(I32), 0)
            return t

        def load_plane(queue, t, src, quadrants=range(4)):
            for q in quadrants:
                queue.dma_start(t[32 * q : 32 * q + 4, :].bitcast(I32), src[0, 4 * q : 4 * q + 4, :].bitcast(I32))

        def load_stage(queue, src, name):
            t = sb.tile([4, 4, R // 4], I32, name=name, align_bytes=64)
            queue.dma_start(t[:], src[0].bitcast(I32).rearrange("(q r) c -> r q c", r=4))
            return t

        def dealt_plane(plane, name):
            t = sb.tile([P, R], U8, name=name, align_bytes=64)
            nc.vector.tensor_copy(t[:].rearrange("p (t m) -> p m t", t=PACK), plane[:].rearrange("p (m t) -> p m t", t=PACK))
            return t

        def words32(src):
            return src[0].rearrange("p n t -> p (n t)").bitcast(I32)

        xt_s = shared.tile([P, T], U8, name="xt_s", offset=3584, align_bytes=64)
        nc.vector.memset(xt_s[:].bitcast(I32), 0)
        xo_s = zeroed_plane(Z, "xo_s")
        w2_s = shared.tile([P, R], U8, name="w2_s", offset=8960, align_bytes=64)
        nc.vector.memset(w2_s[:].bitcast(I32), 0)
        w_s = zeroed_plane(R, "w_s")

        l1 = load_list(offs, "l1")
        w_stage = load_stage(nc.scalar, w_scales, "w_stage")
        l2 = load_list(offs2, "l2")
        xt_w = sb.tile([P, T], U32, name="xt_w", align_bytes=64)
        nc.sync.dma_start(xt_w[:].bitcast(I32), words32(xt_words))
        w_w = sb.tile([P, R], U16, name="w_w", align_bytes=64)
        nc.sync.dma_start(w_w[:].bitcast(I32), w_words[0].bitcast(I32))
        load_plane(nc.sync, xt_s, xt_scales)
        l3 = load_list(offs3, "l3")
        xo_w = sb.tile([P, Z], U16, name="xo_w", align_bytes=64)
        nc.gpsimd.dma_start(xo_w[:].bitcast(I32), xo_words[0].bitcast(I32))
        w2_w = sb.tile([P, R], U32, name="w2_w", align_bytes=64)
        nc.gpsimd.dma_start(w2_w[:].bitcast(I32), words32(w2_words))
        load_plane(nc.sync, xo_s, xo_scales)
        load_plane(nc.sync, w2_s, w2_scales)
        l4 = load_list(offs4, "l4")
        l5 = load_list(offs5, "l5")
        l6 = load_list(offs6, "l6")
        l7 = load_list(offs7, "l7")
        wb_w = sb.tile([P, N], U32, name="wb_w", align_bytes=64)
        nc.sync.dma_start(wb_w[:].bitcast(I32), words32(wb_words))

        boards = {}
        for t in (0, 2, 1):
            boards[t] = sb.tile([P, C], F32, name=f"board{t}", tag=f"board{t}", align_bytes=64)
            nc.vector.memset(boards[t][:], 0.0)
        wb_s = zeroed_plane(N, "wb_s")
        load_plane(nc.sync, wb_s, wb_scales)

        for q in range(4):
            nc.vector.tensor_copy(w_s[32 * q : 32 * q + 4, :].bitcast(I32), w_stage[:, q, :])
        w_sp = dealt_plane(w_s, "w_sp")
        w_wp = sb.tile([P, R], U16, name="w_wp", align_bytes=64)
        nc.scalar.copy(w_wp[:].rearrange("p (t m) -> p m t", t=PACK), w_w[:].rearrange("p (m t) -> p m t", t=PACK))

        xt_wg = sb.tile([P, J], U32, name="xt_wg", align_bytes=64)
        nc.vector.tensor_copy(xt_wg[:], xt_w[:].indirect(l1[:]))
        xt_sg = sb.tile([P, J], U8, name="xt_sg", align_bytes=64)
        nc.vector.tensor_copy(xt_sg[:], xt_s[:].indirect(l1[:]))

        xo_wg = shared.tile([P, J], U16, name="xo_wg", offset=3584, align_bytes=64)
        nc.vector.tensor_copy(xo_wg[:], xo_w[:].indirect(l2[:]))
        w2_wp = shared.tile([P, R], U32, name="w2_wp", offset=4352, align_bytes=64)
        nc.vector.tensor_copy(w2_wp[:].rearrange("p (t m) -> p m t", t=PACK), w2_w[:].rearrange("p (m t) -> p m t", t=PACK))
        xo_sg = shared.tile([P, J], U8, name="xo_sg", offset=4096, align_bytes=64)
        nc.vector.tensor_copy(xo_sg[:], xo_s[:].indirect(l2[:]))
        w2_sp = dealt_plane(w2_s, "w2_sp")

        a_sb = {}
        for t in (2, 3, 0, 1):
            acc = psum.tile([P, J], F32, name=f"a_ps{t}", tag=f"bank{t}")
            cols = slice(t * P, (t + 1) * P)
            nc.tensor.matmul_mx(out=acc[:], lhsT=w_wp[:, cols].bitcast(E2M1), lhsT_scale=w_sp[:, cols],
                                rhs=xt_wg[:].bitcast(E4M3), rhs_scale=xt_sg[:], start=True, stop=True)
            if t < 2:
                at = shared.tile([P, J], F32, name=f"a{t}", offset=8192 + 1024 * t, align_bytes=64)
                nc.vector.tensor_copy(at[:], acc[:])
            else:
                at = sb.tile([P, J], F32, name=f"a{t}")
                nc.scalar.copy(at[:], acc[:])
            a_sb[t] = at

        nc.scalar.activation(boards[2][:].indirect(l3[:]), a_sb[2][:], COPY)
        for t in (0, 1):
            nc.vector.tensor_copy(boards[t][:].indirect(l3[:]), a_sb[t][:])

        b_sb = {}
        for t in (2, 0, 1, 3):
            acc = psum.tile([P, J], F32, name=f"b_ps{t}", tag=f"bank{PACK + t}")
            cols = slice(t * P, (t + 1) * P)
            nc.tensor.matmul_mx(out=acc[:], lhsT=w2_wp[:, cols].bitcast(E5M2), lhsT_scale=w2_sp[:, cols],
                                rhs=xo_wg[:].bitcast(E2M1), rhs_scale=xo_sg[:], start=True, stop=True)
            bt = sb.tile([P, J], F32, name=f"b{t}")
            nc.scalar.copy(bt[:], acc[:])
            b_sb[t] = bt

        boards[3] = sb.tile([P, C], F32, name="board3", tag="w2_sp", align_bytes=64)
        nc.gpsimd.memset(boards[3][:], 0.0)
        pages = [shared.tile([P, E], F32, name="page0", offset=4096, align_bytes=64),
                 shared.tile([P, E], F32, name="page1", offset=0, align_bytes=64)]
        for pg in pages:
            nc.gpsimd.memset(pg[:], 0.0)
        nc.vector.tensor_copy(boards[3][:].indirect(l3[:]), a_sb[3][:])

        groups = ((0, 3), (3, 4))
        looks = {}
        for lo, hi in groups:
            for name in ("g4", "g5", "g6"):
                looks[name, lo] = sb.tile([P, hi - lo, O], F32, name=f"{name}_{lo}")

        def slot_look(t):
            lo = t // 3 * 3
            nc.scalar.activation(looks["g6", lo][:, t - lo, :], b_sb[t][:].indirect(l6[:]), COPY, scale=a_sb[t][:, 0:1])

        def board_looks(t):
            lo = t // 3 * 3
            nc.scalar.activation(looks["g4", lo][:, t - lo, :], boards[t][:].indirect(l4[:]), COPY, scale=b_sb[t][:, 0:1])
            nc.scalar.activation(looks["g5", lo][:, t - lo, :], boards[t][:].indirect(l5[:]), COPY, scale=b_sb[t][:, 128:129])

        for t in (2, 0, 1):
            board_looks(t)
            slot_look(t)
        board_looks(3)
        slot_look(3)

        hid = sb.tile([P, O, PACK], BF16, name="hid", align_bytes=64)
        for lo, hi in groups:
            larger = sb.tile([P, hi - lo, O], F32, name=f"larger{lo}", tag="larger")
            nc.vector.tensor_tensor(larger[:], looks["g4", lo][:], looks["g5", lo][:], MAX)
            nc.vector.tensor_tensor(hid[:, :, lo:hi], larger[:].rearrange("p t o -> p o t"),
                                    looks["g6", lo][:].rearrange("p t o -> p o t"), SUB)
        hid_w = sb.tile([P, O], U32, name="hid_w", align_bytes=64)
        hid_s = sb.tile([P, O], U8, name="hid_s", align_bytes=64)
        nc.vector.quantize_mx(out=hid_w[:].bitcast(E4M3), scales=hid_s[:], in_=hid[:].rearrange("p o t -> p (o t)"))

        for h in range(N // P):
            acc = psum.tile([P, O], F32, name=f"p_ps{h}", tag=f"bank{h}")
            cols = slice(h * P, (h + 1) * P)
            nc.tensor.matmul_mx(out=acc[:], lhsT=wb_w[:, cols].bitcast(E5M2), lhsT_scale=wb_s[:, cols],
                                rhs=hid_w[:].bitcast(E4M3), rhs_scale=hid_s[:], start=True, stop=True)
            pt = sb.tile([P, O], F32, name=f"p{h}")
            if h == 0:
                nc.vector.tensor_copy(pt[:], acc[:])
                nc.vector.tensor_copy(pages[h][:].indirect(l7[:]), pt[:])
                nc.sync.dma_start(out[h * P : (h + 1) * P, :], pages[h][:])
            else:
                nc.scalar.copy(pt[:], acc[:])
                nc.scalar.activation(pages[h][:].indirect(l7[:]), pt[:], COPY)
                nc.scalar.dma_start(out[h * P : (h + 1) * P, :], pages[h][:])
